import numpy as np
import ml_dtypes


def mxq(x, axis, fmt="e4m3"):
    dtype, down = {"e4m3": (ml_dtypes.float8_e4m3fn, 7), "e5m2": (ml_dtypes.float8_e5m2, 14)}[fmt]
    v = np.moveaxis(np.asarray(x, np.float32).astype(ml_dtypes.bfloat16).astype(np.float64), axis, -1)
    blocks = v.reshape(v.shape[:-1] + (-1, 32))
    amax = np.abs(blocks).max(-1, keepdims=True)
    byte = np.maximum(np.where(amax > 0, np.frexp(amax)[1] - 1 + 127, 0) - down, 1)
    scale = np.exp2(byte - 127.0)
    codes = (blocks / scale).astype(np.float32).astype(dtype).astype(np.float64)
    return np.moveaxis((codes * scale).reshape(v.shape), -1, axis)


WIDE = False


def mx_kscale(k):
    if not WIDE:
        return np.ones(k)
    levels = np.array([30, -30])
    if k % 512:
        return np.exp2(np.random.permutation(np.resize(levels, k // 32))).repeat(32)
    a = np.empty((k // 512, 16))
    for p in range(k // 512):
        a[p, :8] = np.random.permutation(np.resize(levels, 8))
        for g in range(8):
            far = levels[np.abs(levels - a[p, g]) >= 10]
            a[p, g + 8] = far[np.random.randint(len(far))]
    return np.exp2(a.ravel()).repeat(32)


def f64(x):
    return np.asarray(x).astype(np.float64)


def striped(idx):
    return np.tile(np.asarray(idx).reshape(-1, 16).T, (8, 1)).astype(np.uint16)


def unstriped(offs):
    return offs[:16].T.reshape(-1).astype(np.int64)


E2M1 = np.array([0.0, 0.5, 1.0, 1.5, 2.0, 3.0, 4.0, 6.0, -0.0, -0.5, -1.0, -1.5, -2.0, -3.0, -4.0, -6.0])


def pack_weight(w, fmt):
    k, n = w.shape
    w = f64(np.asarray(w, np.float32).astype(ml_dtypes.bfloat16)).reshape(k // 32, 32, n)
    amax = np.abs(w).max(1)
    if fmt == "e4m3":
        byte = np.frexp(amax)[1] - 1 + 127 - 7
    else:
        mant, ex = np.frexp(amax / 6.0)
        byte = np.where(mant > 0.5, ex, ex - 1) + 127
    byte = np.clip(np.where(amax > 0, byte, 1), 1, 254)
    scaled = (w * np.exp2(127.0 - byte)[:, None, :]).reshape(k, n).astype(np.float32)
    by_word = np.ascontiguousarray(scaled.reshape(k // 512, 128, 4, n).transpose(0, 1, 3, 2))
    if fmt == "e4m3":
        words = by_word.astype(ml_dtypes.float8_e4m3fn).view(np.uint8)
    else:
        c = by_word.astype(ml_dtypes.float4_e2m1fn).view(np.uint8) & 0xF
        words = (c[..., 0::2] | (c[..., 1::2] << 4)).reshape(k // 512, 128, 2 * n)
    return np.ascontiguousarray(words), np.ascontiguousarray(byte.astype(np.uint8).reshape(k // 512, 16, n))


def unpack_weight(words, scales, fmt):
    g, _, n = scales.shape
    words = np.ascontiguousarray(words).reshape(g, 128, n, -1)
    if fmt == "e4m3":
        vals = words.view(ml_dtypes.float8_e4m3fn).astype(np.float64)
    else:
        nib = np.empty((g, 128, n, 4), np.uint8)
        nib[..., 0::2] = words & 0xF
        nib[..., 1::2] = words >> 4
        vals = E2M1[nib]
    vals = vals * np.repeat(np.exp2(scales.astype(np.float64) - 127.0), 8, axis=1)[..., None]
    return vals.transpose(0, 1, 3, 2).reshape(g * 512, n)


K, T, J, S, R, O, N = 512, 512, 256, 512, 512, 128, 256


def setup_inputs():
    n = np.random.standard_normal
    idx = np.random.permutation(T)[:J]
    idx2 = np.random.permutation(S)[:J]
    idx3 = np.random.permutation(J)[:O]
    idx4 = np.random.permutation(J)[:O]
    fk = mx_kscale(K)
    fr = mx_kscale(R)
    wp = pack_weight(n((K, R)) * 1 / np.sqrt(K) * fk[:, None] * fr, "e2m1")
    wbp = pack_weight(n((R, N)) * 1 / np.sqrt(R) / fr[:, None], "e2m1")
    return {
        "xa": (n((K, T))).astype(np.float32),
        "xb": (n((K, S))).astype(np.float32),
        "hb": (np.random.uniform(0.2, 0.9, (K, 1))).astype(np.float32),
        "fk": (np.random.uniform(0.5, 2.0, (K, 1)) / fk[:, None]).astype(np.float32),
        "w_words": wp[0],
        "w_scales": wp[1],
        "wb_words": wbp[0],
        "wb_scales": wbp[1],
        "rs": (n((N, O))).astype(np.float32),
        "gm": (np.random.uniform(0.5, 2.0, (N, 1))).astype(np.float32),
        "offs": striped(idx),
        "offs2": striped(idx2),
        "offs3": striped(idx3),
        "offs4": striped(idx4),
    }


def reference(xa, xb, hb, fk, w_words, w_scales, wb_words, wb_scales, rs, gm, offs, offs2, offs3, offs4):
    idx = unstriped(offs)
    idx2 = unstriped(offs2)
    idx3 = unstriped(offs3)
    idx4 = unstriped(offs4)
    wu = unpack_weight(w_words, w_scales, "e2m1")
    wbu = unpack_weight(wb_words, wb_scales, "e2m1")
    u = (f64(xa)[:, idx] - np.minimum(f64(xb)[:, idx2], f64(hb))) * f64(fk)
    uq = mxq(u, 0, "e4m3")
    a = wu.T @ uq
    ha = np.maximum(a, 0.0)
    hid = ha[:, idx3] - ha[:, idx4]
    hidq = mxq(hid, 0, "e5m2")
    p = wbu.T @ hidq
    y = f64(gm) * p + f64(rs)
    return y

@@ -1,0 +1,175 @@
+from contextlib import ExitStack
+
+import concourse.mybir as mybir
+
+F32 = mybir.dt.float32
+BF16 = mybir.dt.bfloat16
+I32 = mybir.dt.int32
+U32 = mybir.dt.uint32
+U16 = mybir.dt.uint16
+U8 = mybir.dt.uint8
+E4M3 = mybir.dt.float8_e4m3fn_x4
+E5M2 = mybir.dt.float8_e5m2_x4
+E2M1 = mybir.dt.float4_e2m1fn_x4
+ALU = mybir.AluOpType
+ACT = mybir.ActivationFunctionType
+
+K, T, J, S, R, O, N = 512, 512, 256, 512, 512, 128, 256
+P = 128
+PACK = 4
+HALF = J // 2
+LINE = 4
+
+FLOPS = 2 * K * R * J + 2 * R * N * O
+
+
+def tile_list_looks_boundedgaps_gap_residual_kernel(
+    tc, xa, xb, hb, fk, w_words, w_scales, wb_words, wb_scales, rs, gm, offs, offs2, offs3, offs4, out
+):
+    nc = tc.nc
+    with ExitStack() as ctx:
+        lists = ctx.enter_context(tc.tile_pool(name="lists", bufs=1))
+        sb = ctx.enter_context(tc.tile_pool(name="sb", bufs=1))
+        ps = ctx.enter_context(tc.psum_pool(name="ps", bufs=1))
+
+        idx_a = lists.tile([P, J // 16], U16, name="idx_a")
+        idx_b = lists.tile([P, J // 16], U16, name="idx_b")
+        idx_plus = lists.tile([P, O // 16], U16, name="idx_plus")
+        idx_minus = lists.tile([P, O // 16], U16, name="idx_minus")
+
+        a_rows = xa.rearrange("(p t) c -> p t c", t=PACK)
+        b_rows = xb.rearrange("(p t) c -> p t c", t=PACK)
+        a_sb = [sb.tile([P, T], F32, name="a_sb%d" % t) for t in range(PACK)]
+        b_sb = [sb.tile([P, S], F32, name="b_sb%d" % t) for t in range(PACK)]
+        bound = sb.tile([P, PACK], F32, name="bound")
+        factor = sb.tile([P, PACK], F32, name="factor")
+        w_raw = sb.tile([P, 2 * R], U8, name="w_raw", align_bytes=64)
+        ws_raw = sb.tile([P, R], U8, name="ws_raw", align_bytes=64)
+        wb_sb = sb.tile([P, 2 * N], U8, name="wb_sb", align_bytes=64)
+        wbs_sb = sb.tile([P, N], U8, name="wbs_sb", align_bytes=64)
+        rs_sb = sb.tile([P, N // P, O], F32, name="rs_sb")
+        gain = sb.tile([P, N // P], F32, name="gain")
+
+        nc.vector.memset(ws_raw[:].bitcast(U32), 0)
+        nc.gpsimd.memset(wbs_sb[:].bitcast(U32), 0)
+
+        nc.sync.dma_start(idx_b[:], offs2)
+        for q in range(4):
+            nc.scalar.dma_start(
+                ws_raw[32 * q : 32 * q + 4, :].bitcast(I32), w_scales[0, 4 * q : 4 * q + 4, :].bitcast(I32)
+            )
+        nc.sync.dma_start(b_sb[0][:], b_rows[:, 0, :])
+        nc.sync.dma_start(a_sb[0][:], a_rows[:, 0, :])
+        nc.sync.dma_start(b_sb[1][:], b_rows[:, 1, :])
+        nc.sync.dma_start(idx_a[:], offs)
+        nc.sync.dma_start(bound[:], hb.rearrange("(p t) o -> p (t o)", t=PACK))
+        nc.sync.dma_start(factor[:], fk.rearrange("(p t) o -> p (t o)", t=PACK))
+        nc.sync.dma_start(a_sb[1][:], a_rows[:, 1, :])
+        nc.sync.dma_start(w_raw[:].bitcast(I32), w_words[0].bitcast(I32))
+        for t in range(2, PACK):
+            nc.sync.dma_start(b_sb[t][:], b_rows[:, t, :])
+            nc.sync.dma_start(a_sb[t][:], a_rows[:, t, :])
+        nc.sync.dma_start(idx_plus[:], offs3)
+        nc.sync.dma_start(idx_minus[:], offs4)
+        nc.sync.dma_start(wb_sb[:].bitcast(I32), wb_words[0].bitcast(I32))
+        for q in range(4):
+            nc.sync.dma_start(
+                wbs_sb[32 * q : 32 * q + 4, :].bitcast(I32), wb_scales[0, 4 * q : 4 * q + 4, :].bitcast(I32)
+            )
+        nc.sync.dma_start(rs_sb[:], rs.rearrange("(c p) o -> p c o", p=P))
+        with nc.allow_non_contiguous_dma(reason="one factor for each output row"):
+            nc.sync.dma_start(gain[:], gm.rearrange("(c p) o -> p (c o)", p=P))
+
+        w_dealt = sb.tile([P, 2 * R], U8, name="w_dealt", align_bytes=64)
+        ws_dealt = sb.tile([P, R], U8, name="ws_dealt", align_bytes=64)
+        nc.vector.tensor_copy(
+            ws_dealt[:].rearrange("p (t m) -> p t m", t=PACK),
+            ws_raw[:].rearrange("p (m t) -> p t m", t=PACK),
+        )
+
+        u = sb.tile([P, J, PACK], BF16, name="u", align_bytes=64)
+        halves = [slice(h * HALF, (h + 1) * HALF) for h in range(2)]
+        list_halves = [slice(h * HALF // 16, (h + 1) * HALF // 16) for h in range(2)]
+        for t in range(PACK):
+            gb = sb.tile([P, J], F32, name="gb%d" % t)
+            ga = sb.tile([P, J], F32, name="ga%d" % t)
+            gap = sb.tile([P, J], F32, name="gap%d" % t)
+            if t == 0:
+                nc.vector.tensor_copy(gb[:], b_sb[t][:].indirect(idx_b[:]))
+            else:
+                nc.scalar.activation(gb[:], b_sb[t][:].indirect(idx_b[:]), ACT.Copy)
+            nc.vector.tensor_copy(ga[:, halves[0]], a_sb[t][:].indirect(idx_a[:, list_halves[0]]))
+            nc.scalar.activation(ga[:, halves[1]], a_sb[t][:].indirect(idx_a[:, list_halves[1]]), ACT.Copy)
+            pieces = halves if t == PACK - 1 else [slice(0, J)]
+            for cols in pieces:
+                nc.vector.scalar_tensor_tensor(
+                    gap[:, cols], gb[:, cols], bound[:, t : t + 1], ga[:, cols], ALU.min, ALU.subtract
+                )
+            for cols in pieces:
+                nc.vector.tensor_scalar(u[:, cols, t], gap[:, cols], factor[:, t : t + 1], -1.0, ALU.mult, ALU.mult)
+            if t == 1:
+                nc.vector.tensor_copy(
+                    w_dealt[:].bitcast(U16).rearrange("p (t m) -> p t m", t=PACK),
+                    w_raw[:].bitcast(U16).rearrange("p (m t) -> p t m", t=PACK),
+                )
+        u_codes = [sb.tile([P, HALF], U32, name="u_codes%d" % h, align_bytes=64) for h in range(2)]
+        u_scales = [sb.tile([P, HALF], U8, name="u_scales%d" % h, align_bytes=64) for h in range(2)]
+        for h in range(2):
+            nc.vector.quantize_mx(
+                u_codes[h][:].bitcast(E4M3),
+                u_scales[h][:],
+                u[:, h * HALF : (h + 1) * HALF, :].rearrange("p j t -> p (j t)"),
+            )
+
+        acc = [ps.tile([P, J], F32, name="acc%d" % t) for t in range(PACK)]
+        for h in range(2):
+            for t in range(PACK):
+                nc.tensor.matmul_mx(
+                    acc[t][:, h * HALF : (h + 1) * HALF],
+                    lhsT=w_dealt[:, 2 * P * t : 2 * P * (t + 1)].bitcast(E2M1),
+                    lhsT_scale=ws_dealt[:, P * t : P * (t + 1)],
+                    rhs=u_codes[h][:].bitcast(E4M3),
+                    rhs_scale=u_scales[h][:],
+                    start=True,
+                    stop=True,
+                )
+
+        ha = [sb.tile([P, J], F32, name="ha%d" % t) for t in range(PACK)]
+        for t in range(PACK):
+            if t % 2 == 0:
+                nc.scalar.activation(ha[t][:], acc[t][:], ACT.Relu)
+            else:
+                nc.vector.tensor_scalar(ha[t][:], acc[t][:], 0.0, None, ALU.max)
+
+        plus = sb.tile([P, PACK, O], F32, name="plus")
+        minus = sb.tile([P, PACK, O], F32, name="minus")
+        for t in range(PACK):
+            nc.vector.tensor_copy(plus[:, t, :], ha[t][:].indirect(idx_plus[:]))
+            nc.scalar.activation(minus[:, t, :], ha[t][:].indirect(idx_minus[:]), ACT.Copy)
+
+        hid = sb.tile([P, O, PACK], BF16, name="hid", align_bytes=64)
+        nc.vector.tensor_tensor(
+            hid[:].rearrange("p (c i) t -> p c t i", i=LINE),
+            plus[:].rearrange("p t (c i) -> p c t i", i=LINE),
+            minus[:].rearrange("p t (c i) -> p c t i", i=LINE),
+            ALU.subtract,
+        )
+        hid_codes = sb.tile([P, O], U32, name="hid_codes", align_bytes=64)
+        hid_scales = sb.tile([P, O], U8, name="hid_scales", align_bytes=64)
+        nc.vector.quantize_mx(hid_codes[:].bitcast(E5M2), hid_scales[:], hid[:].rearrange("p o t -> p (o t)"))
+
+        for c in range(N // P):
+            prod = ps.tile([P, O], F32, name="prod%d" % c)
+            nc.tensor.matmul_mx(
+                prod[:],
+                lhsT=wb_sb[:, 2 * P * c : 2 * P * (c + 1)].bitcast(E2M1),
+                lhsT_scale=wbs_sb[:, P * c : P * (c + 1)],
+                rhs=hid_codes[:].bitcast(E5M2),
+                rhs_scale=hid_scales[:],
+                start=True,
+                stop=True,
+            )
+            res = sb.tile([P, O], F32, name="res%d" % c)
+            nc.vector.scalar_tensor_tensor(res[:], prod[:], gain[:, c : c + 1], rs_sb[:, c, :], ALU.mult, ALU.add)
+            queue = nc.sync if c == 0 else nc.scalar
+            queue.dma_start(out[P * c : P * (c + 1), :], res[:])

@@ -44,74 +44,94 @@ def tile_list_looks_boundedgaps_gap_residual_kernel(
         bound = sb.tile([P, PACK], F32, name="bound")
         factor = sb.tile([P, PACK], F32, name="factor")
         w_raw = sb.tile([P, 2 * R], U8, name="w_raw", align_bytes=64)
-        ws_raw = sb.tile([P, R], U8, name="ws_raw", align_bytes=64)
+        ws_raw = sb.tile([P, R], U8, name="ws_raw", tag="reused", align_bytes=64)
         wb_sb = sb.tile([P, 2 * N], U8, name="wb_sb", align_bytes=64)
         wbs_sb = sb.tile([P, N], U8, name="wbs_sb", align_bytes=64)
         rs_sb = sb.tile([P, N // P, O], F32, name="rs_sb")
         gain = sb.tile([P, N // P], F32, name="gain")
 
-        nc.vector.memset(ws_raw[:].bitcast(U32), 0)
+        warm_in = sb.tile([P, 1], F32, name="warm_in")
+        warm_out = sb.tile([P, 1], F32, name="warm_out")
+        nc.vector.memset(warm_in[:], 0.0)
+        nc.scalar.activation(warm_out[:], warm_in[:], ACT.Relu)
+        nc.gpsimd.memset(ws_raw[:].bitcast(U32), 0)
         nc.gpsimd.memset(wbs_sb[:].bitcast(U32), 0)
 
-        nc.sync.dma_start(idx_b[:], offs2)
-        for q in range(4):
-            nc.scalar.dma_start(
-                ws_raw[32 * q : 32 * q + 4, :].bitcast(I32), w_scales[0, 4 * q : 4 * q + 4, :].bitcast(I32)
-            )
-        nc.sync.dma_start(b_sb[0][:], b_rows[:, 0, :])
-        nc.sync.dma_start(a_sb[0][:], a_rows[:, 0, :])
-        nc.sync.dma_start(b_sb[1][:], b_rows[:, 1, :])
+        def load_scale_rows(queue, plane, scales, q):
+            queue.dma_start(plane[32 * q : 32 * q + 4, :].bitcast(I32), scales[0, 4 * q : 4 * q + 4, :].bitcast(I32))
+
         nc.sync.dma_start(idx_a[:], offs)
+        nc.sync.dma_start(a_sb[0][:], a_rows[:, 0, :])
+        nc.sync.dma_start(w_raw[:].bitcast(I32), w_words[0].bitcast(I32))
+        nc.sync.dma_start(idx_b[:], offs2)
+        nc.sync.dma_start(b_sb[0][:], b_rows[:, 0, :])
         nc.sync.dma_start(bound[:], hb.rearrange("(p t) o -> p (t o)", t=PACK))
         nc.sync.dma_start(factor[:], fk.rearrange("(p t) o -> p (t o)", t=PACK))
-        nc.sync.dma_start(a_sb[1][:], a_rows[:, 1, :])
-        nc.sync.dma_start(w_raw[:].bitcast(I32), w_words[0].bitcast(I32))
-        for t in range(2, PACK):
-            nc.sync.dma_start(b_sb[t][:], b_rows[:, t, :])
+        for t in range(1, PACK):
             nc.sync.dma_start(a_sb[t][:], a_rows[:, t, :])
+            nc.sync.dma_start(b_sb[t][:], b_rows[:, t, :])
+        for q in range(4):
+            load_scale_rows(nc.sync, ws_raw, w_scales, q)
         nc.sync.dma_start(idx_plus[:], offs3)
         nc.sync.dma_start(idx_minus[:], offs4)
         nc.sync.dma_start(wb_sb[:].bitcast(I32), wb_words[0].bitcast(I32))
         for q in range(4):
-            nc.sync.dma_start(
-                wbs_sb[32 * q : 32 * q + 4, :].bitcast(I32), wb_scales[0, 4 * q : 4 * q + 4, :].bitcast(I32)
-            )
+            load_scale_rows(nc.sync, wbs_sb, wb_scales, q)
         nc.sync.dma_start(rs_sb[:], rs.rearrange("(c p) o -> p c o", p=P))
         with nc.allow_non_contiguous_dma(reason="one factor for each output row"):
             nc.sync.dma_start(gain[:], gm.rearrange("(c p) o -> p (c o)", p=P))
 
         w_dealt = sb.tile([P, 2 * R], U8, name="w_dealt", align_bytes=64)
         ws_dealt = sb.tile([P, R], U8, name="ws_dealt", align_bytes=64)
+        u = sb.tile([P, J, PACK], BF16, name="u", align_bytes=64)
+        whole = slice(0, J)
+        halves = [slice(h * HALF, (h + 1) * HALF) for h in range(2)]
+        gb = [sb.tile([P, J], F32, name="gb%d" % t) for t in range(PACK)]
+        ga = [sb.tile([P, J], F32, name="ga%d" % t) for t in range(PACK)]
+        gap = [sb.tile([P, J], F32, name="gap%d" % t) for t in range(PACK - 1)]
+
+        def entries(cols):
+            return slice(cols.start // 16, cols.stop // 16)
+
+        def pick_scalar(dst, table, idx, cols):
+            nc.scalar.activation(dst[:, cols], table[:].indirect(idx[:, entries(cols)]), ACT.Copy)
+
+        def pick_vector(dst, table, idx, cols):
+            nc.vector.tensor_copy(dst[:, cols], table[:].indirect(idx[:, entries(cols)]))
+
+        def pick_both(dst, table, idx, cut):
+            pick_vector(dst, table, idx, slice(0, cut))
+            pick_scalar(dst, table, idx, slice(cut, J))
+
+        def subtract(t, cols):
+            nc.vector.scalar_tensor_tensor(
+                gap[t][:, cols], gb[t][:, cols], bound[:, t : t + 1], ga[t][:, cols], ALU.min, ALU.subtract
+            )
+
+        def scale(t, cols):
+            nc.vector.tensor_scalar(u[:, cols, t], gap[t][:, cols], factor[:, t : t + 1], -1.0, ALU.mult, ALU.mult)
+
+        pick_both(ga[0], a_sb[0], idx_a, 128)
+        nc.vector.tensor_copy(
+            w_dealt[:].bitcast(U16).rearrange("p (t m) -> p t m", t=PACK),
+            w_raw[:].bitcast(U16).rearrange("p (m t) -> p t m", t=PACK),
+        )
+        pick_both(gb[0], b_sb[0], idx_b, 128)
+        for t in range(PACK - 1):
+            subtract(t, whole)
+            pick_both(ga[t + 1], a_sb[t + 1], idx_a, 96)
+            scale(t, whole)
+            for cols in halves if t + 1 == PACK - 1 else [whole]:
+                pick_scalar(gb[t + 1], b_sb[t + 1], idx_b, cols)
         nc.vector.tensor_copy(
             ws_dealt[:].rearrange("p (t m) -> p t m", t=PACK),
             ws_raw[:].rearrange("p (m t) -> p t m", t=PACK),
         )
-
-        u = sb.tile([P, J, PACK], BF16, name="u", align_bytes=64)
-        halves = [slice(h * HALF, (h + 1) * HALF) for h in range(2)]
-        list_halves = [slice(h * HALF // 16, (h + 1) * HALF // 16) for h in range(2)]
-        for t in range(PACK):
-            gb = sb.tile([P, J], F32, name="gb%d" % t)
-            ga = sb.tile([P, J], F32, name="ga%d" % t)
-            gap = sb.tile([P, J], F32, name="gap%d" % t)
-            if t == 0:
-                nc.vector.tensor_copy(gb[:], b_sb[t][:].indirect(idx_b[:]))
-            else:
-                nc.scalar.activation(gb[:], b_sb[t][:].indirect(idx_b[:]), ACT.Copy)
-            nc.vector.tensor_copy(ga[:, halves[0]], a_sb[t][:].indirect(idx_a[:, list_halves[0]]))
-            nc.scalar.activation(ga[:, halves[1]], a_sb[t][:].indirect(idx_a[:, list_halves[1]]), ACT.Copy)
-            pieces = halves if t == PACK - 1 else [slice(0, J)]
-            for cols in pieces:
-                nc.vector.scalar_tensor_tensor(
-                    gap[:, cols], gb[:, cols], bound[:, t : t + 1], ga[:, cols], ALU.min, ALU.subtract
-                )
-            for cols in pieces:
-                nc.vector.tensor_scalar(u[:, cols, t], gap[:, cols], factor[:, t : t + 1], -1.0, ALU.mult, ALU.mult)
-            if t == 1:
-                nc.vector.tensor_copy(
-                    w_dealt[:].bitcast(U16).rearrange("p (t m) -> p t m", t=PACK),
-                    w_raw[:].bitcast(U16).rearrange("p (m t) -> p t m", t=PACK),
-                )
+        gap.append(sb.tile([P, J], F32, name="gap_last", tag="reused", align_bytes=64))
+        for cols in halves:
+            subtract(3, cols)
+        for cols in halves:
+            scale(3, cols)
         u_codes = [sb.tile([P, HALF], U32, name="u_codes%d" % h, align_bytes=64) for h in range(2)]
         u_scales = [sb.tile([P, HALF], U8, name="u_scales%d" % h, align_bytes=64) for h in range(2)]
         for h in range(2):
@@ -122,8 +142,8 @@ def tile_list_looks_boundedgaps_gap_residual_kernel(
             )
 
         acc = [ps.tile([P, J], F32, name="acc%d" % t) for t in range(PACK)]
-        for h in range(2):
-            for t in range(PACK):
+        if True:
+            for h, t in [(0, 0), (0, 1), (1, 0), (1, 1), (0, 2), (1, 2), (0, 3), (1, 3)]:
                 nc.tensor.matmul_mx(
                     acc[t][:, h * HALF : (h + 1) * HALF],
                     lhsT=w_dealt[:, 2 * P * t : 2 * P * (t + 1)].bitcast(E2M1),
@@ -145,7 +165,10 @@ def tile_list_looks_boundedgaps_gap_residual_kernel(
         minus = sb.tile([P, PACK, O], F32, name="minus")
         for t in range(PACK):
             nc.vector.tensor_copy(plus[:, t, :], ha[t][:].indirect(idx_plus[:]))
-            nc.scalar.activation(minus[:, t, :], ha[t][:].indirect(idx_minus[:]), ACT.Copy)
+            if True:
+                nc.scalar.activation(minus[:, t, :], ha[t][:].indirect(idx_minus[:]), ACT.Copy)
+            else:
+                nc.vector.tensor_copy(minus[:, t, :], ha[t][:].indirect(idx_minus[:]))
 
         hid = sb.tile([P, O, PACK], BF16, name="hid", align_bytes=64)
         nc.vector.tensor_tensor(

@@ -18,7 +18,7 @@ K, T, J, S, R, O, N = 512, 512, 256, 512, 512, 128, 256
 P = 128
 PACK = 4
 HALF = J // 2
-LINE = 4
+LINE = 2
 
 FLOPS = 2 * K * R * J + 2 * R * N * O
 
@@ -44,16 +44,12 @@ def tile_list_looks_boundedgaps_gap_residual_kernel(
         bound = sb.tile([P, PACK], F32, name="bound")
         factor = sb.tile([P, PACK], F32, name="factor")
         w_raw = sb.tile([P, 2 * R], U8, name="w_raw", align_bytes=64)
-        ws_raw = sb.tile([P, R], U8, name="ws_raw", tag="reused", align_bytes=64)
+        ws_raw = sb.tile([P, R], U8, name="ws_raw", align_bytes=64)
         wb_sb = sb.tile([P, 2 * N], U8, name="wb_sb", align_bytes=64)
         wbs_sb = sb.tile([P, N], U8, name="wbs_sb", align_bytes=64)
         rs_sb = sb.tile([P, N // P, O], F32, name="rs_sb")
         gain = sb.tile([P, N // P], F32, name="gain")
 
-        warm_in = sb.tile([P, 1], F32, name="warm_in")
-        warm_out = sb.tile([P, 1], F32, name="warm_out")
-        nc.vector.memset(warm_in[:], 0.0)
-        nc.scalar.activation(warm_out[:], warm_in[:], ACT.Relu)
         nc.gpsimd.memset(ws_raw[:].bitcast(U32), 0)
         nc.gpsimd.memset(wbs_sb[:].bitcast(U32), 0)
 
@@ -62,11 +58,15 @@ def tile_list_looks_boundedgaps_gap_residual_kernel(
 
         nc.sync.dma_start(idx_a[:], offs)
         nc.sync.dma_start(a_sb[0][:], a_rows[:, 0, :])
-        nc.sync.dma_start(w_raw[:].bitcast(I32), w_words[0].bitcast(I32))
+        nc.scalar.dma_start(w_raw[:].bitcast(I32), w_words[0].bitcast(I32))
         nc.sync.dma_start(idx_b[:], offs2)
         nc.sync.dma_start(b_sb[0][:], b_rows[:, 0, :])
-        nc.sync.dma_start(bound[:], hb.rearrange("(p t) o -> p (t o)", t=PACK))
-        nc.sync.dma_start(factor[:], fk.rearrange("(p t) o -> p (t o)", t=PACK))
+        nc.scalar.dma_start(bound[:], hb.rearrange("(p t) o -> p (t o)", t=PACK))
+        nc.scalar.dma_start(factor[:], fk.rearrange("(p t) o -> p (t o)", t=PACK))
+        warm_in = sb.tile([P, 1], F32, name="warm_in")
+        warm_out = sb.tile([P, 1], F32, name="warm_out")
+        nc.vector.memset(warm_in[:], 0.0)
+        nc.scalar.activation(warm_out[:], warm_in[:], ACT.Relu)
         for t in range(1, PACK):
             nc.sync.dma_start(a_sb[t][:], a_rows[:, t, :])
             nc.sync.dma_start(b_sb[t][:], b_rows[:, t, :])
@@ -82,13 +82,13 @@ def tile_list_looks_boundedgaps_gap_residual_kernel(
             nc.sync.dma_start(gain[:], gm.rearrange("(c p) o -> p (c o)", p=P))
 
         w_dealt = sb.tile([P, 2 * R], U8, name="w_dealt", align_bytes=64)
-        ws_dealt = sb.tile([P, R], U8, name="ws_dealt", align_bytes=64)
+        ws_dealt = [sb.tile([P, P], U8, name="ws_dealt%d" % t, align_bytes=64) for t in range(PACK)]
         u = sb.tile([P, J, PACK], BF16, name="u", align_bytes=64)
         whole = slice(0, J)
         halves = [slice(h * HALF, (h + 1) * HALF) for h in range(2)]
         gb = [sb.tile([P, J], F32, name="gb%d" % t) for t in range(PACK)]
         ga = [sb.tile([P, J], F32, name="ga%d" % t) for t in range(PACK)]
-        gap = [sb.tile([P, J], F32, name="gap%d" % t) for t in range(PACK - 1)]
+        gap = [sb.tile([P, J], F32, name="gap%d" % t) for t in range(PACK)]
 
         def entries(cols):
             return slice(cols.start // 16, cols.stop // 16)
@@ -123,11 +123,6 @@ def tile_list_looks_boundedgaps_gap_residual_kernel(
             scale(t, whole)
             for cols in halves if t + 1 == PACK - 1 else [whole]:
                 pick_scalar(gb[t + 1], b_sb[t + 1], idx_b, cols)
-        nc.vector.tensor_copy(
-            ws_dealt[:].rearrange("p (t m) -> p t m", t=PACK),
-            ws_raw[:].rearrange("p (m t) -> p t m", t=PACK),
-        )
-        gap.append(sb.tile([P, J], F32, name="gap_last", tag="reused", align_bytes=64))
         for cols in halves:
             subtract(3, cols)
         for cols in halves:
@@ -141,13 +136,16 @@ def tile_list_looks_boundedgaps_gap_residual_kernel(
                 u[:, h * HALF : (h + 1) * HALF, :].rearrange("p j t -> p (j t)"),
             )
 
+        for t in range(PACK):
+            nc.vector.tensor_copy(ws_dealt[t][:], ws_raw[:].rearrange("p (m t) -> p t m", t=PACK)[:, t, :])
+
         acc = [ps.tile([P, J], F32, name="acc%d" % t) for t in range(PACK)]
-        if True:
-            for h, t in [(0, 0), (0, 1), (1, 0), (1, 1), (0, 2), (1, 2), (0, 3), (1, 3)]:
+        for t in range(PACK):
+            for h in range(2):
                 nc.tensor.matmul_mx(
                     acc[t][:, h * HALF : (h + 1) * HALF],
                     lhsT=w_dealt[:, 2 * P * t : 2 * P * (t + 1)].bitcast(E2M1),
-                    lhsT_scale=ws_dealt[:, P * t : P * (t + 1)],
+                    lhsT_scale=ws_dealt[t][:],
                     rhs=u_codes[h][:].bitcast(E4M3),
                     rhs_scale=u_scales[h][:],
                     start=True,
@@ -156,19 +154,19 @@ def tile_list_looks_boundedgaps_gap_residual_kernel(
 
         ha = [sb.tile([P, J], F32, name="ha%d" % t) for t in range(PACK)]
         for t in range(PACK):
-            if t % 2 == 0:
+            if t != 1:
                 nc.scalar.activation(ha[t][:], acc[t][:], ACT.Relu)
             else:
                 nc.vector.tensor_scalar(ha[t][:], acc[t][:], 0.0, None, ALU.max)
 
         plus = sb.tile([P, PACK, O], F32, name="plus")
         minus = sb.tile([P, PACK, O], F32, name="minus")
-        for t in range(PACK):
-            nc.vector.tensor_copy(plus[:, t, :], ha[t][:].indirect(idx_plus[:]))
-            if True:
-                nc.scalar.activation(minus[:, t, :], ha[t][:].indirect(idx_minus[:]), ACT.Copy)
+        lookups = [(t, dst, idx) for t in range(PACK) for dst, idx in ((plus, idx_plus), (minus, idx_minus))]
+        for n, (t, dst, idx) in enumerate(lookups):
+            if n < 5:
+                nc.vector.tensor_copy(dst[:, t, :], ha[t][:].indirect(idx[:]))
             else:
-                nc.vector.tensor_copy(minus[:, t, :], ha[t][:].indirect(idx_minus[:]))
+                nc.scalar.activation(dst[:, t, :], ha[t][:].indirect(idx[:]), ACT.Copy)
 
         hid = sb.tile([P, O, PACK], BF16, name="hid", align_bytes=64)
         nc.vector.tensor_tensor(

from contextlib import ExitStack

import concourse.mybir as mybir

F32 = mybir.dt.float32
BF16 = mybir.dt.bfloat16
I32 = mybir.dt.int32
U32 = mybir.dt.uint32
U16 = mybir.dt.uint16
U8 = mybir.dt.uint8
E4M3 = mybir.dt.float8_e4m3fn_x4
E5M2 = mybir.dt.float8_e5m2_x4
E2M1 = mybir.dt.float4_e2m1fn_x4
ALU = mybir.AluOpType
ACT = mybir.ActivationFunctionType

K, T, J, S, R, O, N = 512, 512, 256, 512, 512, 128, 256
P = 128
PACK = 4
HALF = J // 2
LINE = 2

FLOPS = 2 * K * R * J + 2 * R * N * O


def tile_list_looks_boundedgaps_gap_residual_kernel(
    tc, xa, xb, hb, fk, w_words, w_scales, wb_words, wb_scales, rs, gm, offs, offs2, offs3, offs4, out
):
    nc = tc.nc
    with ExitStack() as ctx:
        lists = ctx.enter_context(tc.tile_pool(name="lists", bufs=1))
        sb = ctx.enter_context(tc.tile_pool(name="sb", bufs=1))
        ps = ctx.enter_context(tc.psum_pool(name="ps", bufs=1))

        idx_a = lists.tile([P, J // 16], U16, name="idx_a")
        idx_b = lists.tile([P, J // 16], U16, name="idx_b")
        idx_plus = lists.tile([P, O // 16], U16, name="idx_plus")
        idx_minus = lists.tile([P, O // 16], U16, name="idx_minus")

        a_rows = xa.rearrange("(p t) c -> p t c", t=PACK)
        b_rows = xb.rearrange("(p t) c -> p t c", t=PACK)
        a_sb = [sb.tile([P, T], F32, name="a_sb%d" % t) for t in range(PACK)]
        b_sb = [sb.tile([P, S], F32, name="b_sb%d" % t) for t in range(PACK)]
        bound = sb.tile([P, PACK], F32, name="bound")
        factor = sb.tile([P, PACK], F32, name="factor")
        w_raw = sb.tile([P, 2 * R], U8, name="w_raw", align_bytes=64)
        ws_raw = sb.tile([P, R], U8, name="ws_raw", align_bytes=64)
        wb_sb = sb.tile([P, 2 * N], U8, name="wb_sb", align_bytes=64)
        wbs_sb = sb.tile([P, N], U8, name="wbs_sb", align_bytes=64)
        rs_sb = sb.tile([P, N // P, O], F32, name="rs_sb")
        gain = sb.tile([P, N // P], F32, name="gain")

        nc.gpsimd.memset(ws_raw[:].bitcast(U32), 0)
        nc.gpsimd.memset(wbs_sb[:].bitcast(U32), 0)

        def load_scale_rows(queue, plane, scales, q):
            queue.dma_start(plane[32 * q : 32 * q + 4, :].bitcast(I32), scales[0, 4 * q : 4 * q + 4, :].bitcast(I32))

        nc.sync.dma_start(idx_a[:], offs)
        nc.sync.dma_start(a_sb[0][:], a_rows[:, 0, :])
        nc.scalar.dma_start(w_raw[:].bitcast(I32), w_words[0].bitcast(I32))
        nc.sync.dma_start(idx_b[:], offs2)
        nc.sync.dma_start(b_sb[0][:], b_rows[:, 0, :])
        nc.scalar.dma_start(bound[:], hb.rearrange("(p t) o -> p (t o)", t=PACK))
        nc.scalar.dma_start(factor[:], fk.rearrange("(p t) o -> p (t o)", t=PACK))
        warm_in = sb.tile([P, 1], F32, name="warm_in")
        warm_out = sb.tile([P, 1], F32, name="warm_out")
        nc.vector.memset(warm_in[:], 0.0)
        nc.scalar.activation(warm_out[:], warm_in[:], ACT.Relu)
        for t in range(1, PACK):
            nc.sync.dma_start(a_sb[t][:], a_rows[:, t, :])
            nc.sync.dma_start(b_sb[t][:], b_rows[:, t, :])
        for q in range(4):
            load_scale_rows(nc.sync, ws_raw, w_scales, q)
        nc.sync.dma_start(idx_plus[:], offs3)
        nc.sync.dma_start(idx_minus[:], offs4)
        nc.sync.dma_start(wb_sb[:].bitcast(I32), wb_words[0].bitcast(I32))
        for q in range(4):
            load_scale_rows(nc.sync, wbs_sb, wb_scales, q)
        nc.sync.dma_start(rs_sb[:], rs.rearrange("(c p) o -> p c o", p=P))
        with nc.allow_non_contiguous_dma(reason="one factor for each output row"):
            nc.sync.dma_start(gain[:], gm.rearrange("(c p) o -> p (c o)", p=P))

        w_dealt = sb.tile([P, 2 * R], U8, name="w_dealt", align_bytes=64)
        ws_dealt = [sb.tile([P, P], U8, name="ws_dealt%d" % t, align_bytes=64) for t in range(PACK)]
        u = sb.tile([P, J, PACK], BF16, name="u", align_bytes=64)
        whole = slice(0, J)
        halves = [slice(h * HALF, (h + 1) * HALF) for h in range(2)]
        gb = [sb.tile([P, J], F32, name="gb%d" % t) for t in range(PACK)]
        ga = [sb.tile([P, J], F32, name="ga%d" % t) for t in range(PACK)]
        gap = [sb.tile([P, J], F32, name="gap%d" % t) for t in range(PACK)]

        def entries(cols):
            return slice(cols.start // 16, cols.stop // 16)

        def pick_scalar(dst, table, idx, cols):
            nc.scalar.activation(dst[:, cols], table[:].indirect(idx[:, entries(cols)]), ACT.Copy)

        def pick_vector(dst, table, idx, cols):
            nc.vector.tensor_copy(dst[:, cols], table[:].indirect(idx[:, entries(cols)]))

        def pick_both(dst, table, idx, cut):
            pick_vector(dst, table, idx, slice(0, cut))
            pick_scalar(dst, table, idx, slice(cut, J))

        def subtract(t, cols):
            nc.vector.scalar_tensor_tensor(
                gap[t][:, cols], gb[t][:, cols], bound[:, t : t + 1], ga[t][:, cols], ALU.min, ALU.subtract
            )

        def scale(t, cols):
            nc.vector.tensor_scalar(u[:, cols, t], gap[t][:, cols], factor[:, t : t + 1], -1.0, ALU.mult, ALU.mult)

        pick_both(ga[0], a_sb[0], idx_a, 128)
        nc.vector.tensor_copy(
            w_dealt[:].bitcast(U16).rearrange("p (t m) -> p t m", t=PACK),
            w_raw[:].bitcast(U16).rearrange("p (m t) -> p t m", t=PACK),
        )
        pick_both(gb[0], b_sb[0], idx_b, 128)
        for t in range(PACK - 1):
            subtract(t, whole)
            pick_both(ga[t + 1], a_sb[t + 1], idx_a, 96)
            scale(t, whole)
            for cols in halves if t + 1 == PACK - 1 else [whole]:
                pick_scalar(gb[t + 1], b_sb[t + 1], idx_b, cols)
        for cols in halves:
            subtract(3, cols)
        for cols in halves:
            scale(3, cols)
        u_codes = [sb.tile([P, HALF], U32, name="u_codes%d" % h, align_bytes=64) for h in range(2)]
        u_scales = [sb.tile([P, HALF], U8, name="u_scales%d" % h, align_bytes=64) for h in range(2)]
        for h in range(2):
            nc.vector.quantize_mx(
                u_codes[h][:].bitcast(E4M3),
                u_scales[h][:],
                u[:, h * HALF : (h + 1) * HALF, :].rearrange("p j t -> p (j t)"),
            )

        for t in range(PACK):
            nc.vector.tensor_copy(ws_dealt[t][:], ws_raw[:].rearrange("p (m t) -> p t m", t=PACK)[:, t, :])

        acc = [ps.tile([P, J], F32, name="acc%d" % t) for t in range(PACK)]
        for t in range(PACK):
            for h in range(2):
                nc.tensor.matmul_mx(
                    acc[t][:, h * HALF : (h + 1) * HALF],
                    lhsT=w_dealt[:, 2 * P * t : 2 * P * (t + 1)].bitcast(E2M1),
                    lhsT_scale=ws_dealt[t][:],
                    rhs=u_codes[h][:].bitcast(E4M3),
                    rhs_scale=u_scales[h][:],
                    start=True,
                    stop=True,
                )

        ha = [sb.tile([P, J], F32, name="ha%d" % t) for t in range(PACK)]
        for t in range(PACK):
            if t != 1:
                nc.scalar.activation(ha[t][:], acc[t][:], ACT.Relu)
            else:
                nc.vector.tensor_scalar(ha[t][:], acc[t][:], 0.0, None, ALU.max)

        plus = sb.tile([P, PACK, O], F32, name="plus")
        minus = sb.tile([P, PACK, O], F32, name="minus")
        lookups = [(t, dst, idx) for t in range(PACK) for dst, idx in ((plus, idx_plus), (minus, idx_minus))]
        for n, (t, dst, idx) in enumerate(lookups):
            if n < 5:
                nc.vector.tensor_copy(dst[:, t, :], ha[t][:].indirect(idx[:]))
            else:
                nc.scalar.activation(dst[:, t, :], ha[t][:].indirect(idx[:]), ACT.Copy)

        hid = sb.tile([P, O, PACK], BF16, name="hid", align_bytes=64)
        nc.vector.tensor_tensor(
            hid[:].rearrange("p (c i) t -> p c t i", i=LINE),
            plus[:].rearrange("p t (c i) -> p c t i", i=LINE),
            minus[:].rearrange("p t (c i) -> p c t i", i=LINE),
            ALU.subtract,
        )
        hid_codes = sb.tile([P, O], U32, name="hid_codes", align_bytes=64)
        hid_scales = sb.tile([P, O], U8, name="hid_scales", align_bytes=64)
        nc.vector.quantize_mx(hid_codes[:].bitcast(E5M2), hid_scales[:], hid[:].rearrange("p o t -> p (o t)"))

        for c in range(N // P):
            prod = ps.tile([P, O], F32, name="prod%d" % c)
            nc.tensor.matmul_mx(
                prod[:],
                lhsT=wb_sb[:, 2 * P * c : 2 * P * (c + 1)].bitcast(E2M1),
                lhsT_scale=wbs_sb[:, P * c : P * (c + 1)],
                rhs=hid_codes[:].bitcast(E5M2),
                rhs_scale=hid_scales[:],
                start=True,
                stop=True,
            )
            res = sb.tile([P, O], F32, name="res%d" % c)
            nc.vector.scalar_tensor_tensor(res[:], prod[:], gain[:, c : c + 1], rs_sb[:, c, :], ALU.mult, ALU.add)
            queue = nc.sync if c == 0 else nc.scalar
            queue.dma_start(out[P * c : P * (c + 1), :], res[:])
